import numpy as np
import ml_dtypes


def mxq(x, axis, fmt="e4m3"):
    dtype, down = {"e4m3": (ml_dtypes.float8_e4m3fn, 7), "e5m2": (ml_dtypes.float8_e5m2, 14)}[fmt]
    v = np.moveaxis(np.asarray(x, np.float32).astype(ml_dtypes.bfloat16).astype(np.float64), axis, -1)
    blocks = v.reshape(v.shape[:-1] + (-1, 32))
    amax = np.abs(blocks).max(-1, keepdims=True)
    byte = np.maximum(np.where(amax > 0, np.frexp(amax)[1] - 1 + 127, 0) - down, 1)
    scale = np.exp2(byte - 127.0)
    codes = (blocks / scale).astype(np.float32).astype(dtype).astype(np.float64)
    return np.moveaxis((codes * scale).reshape(v.shape), -1, axis)


WIDE = False


def mx_kscale(k):
    if not WIDE:
        return np.ones(k)
    levels = np.array([10, -10, 5, -5, 0])
    if k % 512:
        return np.exp2(np.random.permutation(np.resize(levels, k // 32))).repeat(32)
    a = np.empty((k // 512, 16))
    for p in range(k // 512):
        a[p, :8] = np.random.permutation(np.resize(levels, 8))
        for g in range(8):
            far = levels[np.abs(levels - a[p, g]) >= 10]
            a[p, g + 8] = far[np.random.randint(len(far))]
    return np.exp2(a.ravel()).repeat(32)


BF16 = ml_dtypes.bfloat16


def bf(x):
    return np.asarray(x, np.float32).astype(BF16)


def f64(x):
    return np.asarray(x).astype(np.float64)


E2M1 = np.array([0.0, 0.5, 1.0, 1.5, 2.0, 3.0, 4.0, 6.0, -0.0, -0.5, -1.0, -1.5, -2.0, -3.0, -4.0, -6.0])


def pack_weight(w, fmt):
    k, n = w.shape
    w = f64(bf(w)).reshape(k // 32, 32, n)
    amax = np.abs(w).max(1)
    if fmt == "e4m3":
        byte = np.frexp(amax)[1] - 1 + 127 - 7
    else:
        mant, ex = np.frexp(amax / 6.0)
        byte = np.where(mant > 0.5, ex, ex - 1) + 127
    byte = np.clip(np.where(amax > 0, byte, 1), 1, 254)
    scaled = (w * np.exp2(127.0 - byte)[:, None, :]).reshape(k, n).astype(np.float32)
    by_word = np.ascontiguousarray(scaled.reshape(k // 512, 128, 4, n).transpose(0, 1, 3, 2))
    if fmt == "e4m3":
        words = by_word.astype(ml_dtypes.float8_e4m3fn).view(np.uint8)
    else:
        c = by_word.astype(ml_dtypes.float4_e2m1fn).view(np.uint8) & 0xF
        words = c[..., 0::2] | (c[..., 1::2] << 4)
    return np.ascontiguousarray(words), np.ascontiguousarray(byte.astype(np.uint8).reshape(k // 512, 16, n))


def unpack_weight(words, scales, fmt):
    g, p, n, _ = words.shape
    if fmt == "e4m3":
        vals = np.ascontiguousarray(words).view(ml_dtypes.float8_e4m3fn).astype(np.float64)
    else:
        nib = np.empty((g, p, n, 4), np.uint8)
        nib[..., 0::2] = words & 0xF
        nib[..., 1::2] = words >> 4
        vals = E2M1[nib]
    vals = vals * np.repeat(np.exp2(scales.astype(np.float64) - 127.0), 8, axis=1)[..., None]
    return vals.transpose(0, 1, 3, 2).reshape(g * 512, n)
def pack4(w):
    words, scales = pack_weight(w, "e2m1")
    return words.reshape(words.shape[0], 128, -1), scales


def unpack4(words, scales):
    return unpack_weight(words.reshape(words.shape[0], 128, -1, 2), scales, "e2m1")


OBS, DIM, CHAINS = 4096, 1024, 512


def setup_inputs():
    s = mx_kscale(DIM)
    t = mx_kscale(OBS)
    x = np.random.standard_normal((OBS, DIM))
    theta = 2.0 * np.random.standard_normal((DIM, CHAINS)) / np.sqrt(DIM)
    x4_words, x4_scales = pack4(x.T * s[:, None])
    theta_words, theta_scales = pack4(theta / s[:, None])
    x8_words, x8_scales = pack_weight(x / np.sqrt(OBS) / t[:, None], "e4m3")
    return {"x4_words": x4_words, "x4_scales": x4_scales,
            "theta_words": theta_words, "theta_scales": theta_scales,
            "x8_words": x8_words, "x8_scales": x8_scales,
            "weight": bf(np.random.uniform(0.5, 1.5, OBS) * t),
            "step": bf(np.random.uniform(1.0, 2.0, CHAINS)),
            "mom": bf(0.5 * np.random.standard_normal((DIM, CHAINS)))}


def reference(x4_words, x4_scales, theta_words, theta_scales, x8_words, x8_scales, weight, step, mom):
    a = unpack4(x4_words, x4_scales)
    th = unpack4(theta_words, theta_scales)
    b = unpack_weight(x8_words, x8_scales, "e4m3")
    z = a.T @ th
    r = f64(weight)[:, None] / (1.0 + np.exp(z))
    grad = b.T @ mxq(r, 0, "e4m3")
    return f64(mom) + grad * f64(step)

@@ -1,0 +1,297 @@
+from contextlib import ExitStack
+
+import concourse.mybir as mybir
+
+OBS, DIM, CHAINS = 4096, 1024, 512
+FLOPS = 2 * 2 * OBS * DIM * CHAINS
+
+F32 = mybir.dt.float32
+BF16 = mybir.dt.bfloat16
+I32 = mybir.dt.int32
+U32 = mybir.dt.uint32
+U8 = mybir.dt.uint8
+FP8X4 = mybir.dt.float8_e4m3fn_x4
+FP4X4 = mybir.dt.float4_e2m1fn_x4
+ACT = mybir.ActivationFunctionType
+ALU = mybir.AluOpType
+
+P = 128
+PACK = 4
+K_PASS = P * PACK
+GROUPS = OBS // K_PASS
+DIM_PASSES = DIM // K_PASS
+DIM_TILES = DIM // P
+BANKS = 8
+EARLY_TILES = 5
+EARLY_SCALE_GROUPS = 2
+SPREAD_FROM = 4
+SCALAR_MULS = [0, 3, 2, 2, 2, 2, 2, 0]
+GPSIMD_ADDS = 2
+
+
+def tile_hmc_logistic_kick_s4_kernel(
+    tc, x4_words, x4_scales, theta_words, theta_scales, x8_words, x8_scales, weight, step, mom, out
+):
+    nc = tc.nc
+    with ExitStack() as ctx:
+        keep = ctx.enter_context(tc.tile_pool(name="keep", bufs=1))
+        work = ctx.enter_context(tc.tile_pool(name="work", bufs=1))
+        psum = ctx.enter_context(tc.psum_pool(name="psum", bufs=1))
+        ctx.enter_context(tc.manual_schedule())
+
+        def load_scale_rows(queues, plane, rows):
+            for quad in range(4):
+                queues[quad].dma_start(
+                    out=plane[32 * quad : 32 * quad + 4, :, :].bitcast(I32),
+                    in_=rows[:, 4 * quad : 4 * quad + 4, :].rearrange("k r c -> r k c").bitcast(I32),
+                )
+
+        a_words_i32 = x4_words.bitcast(I32)
+        a_raw = []
+
+        def load_a(g):
+            raw = keep.tile([P, DIM_PASSES, 2 * K_PASS], U8, name="a_raw%d" % g, align_bytes=64)
+            nc.sync.dma_start(
+                out=raw[:].bitcast(I32),
+                in_=a_words_i32[:, :, 256 * g : 256 * (g + 1)].rearrange("k p c -> p k c"),
+            )
+            a_raw.append(raw)
+
+        b_words = []
+
+        def load_b(g):
+            words = keep.tile([P, DIM], U32, name="b_words%d" % g, align_bytes=64)
+            nc.sync.dma_start(
+                out=words[:].bitcast(I32),
+                in_=x8_words[g].rearrange("p n t -> p (n t)").bitcast(I32),
+            )
+            b_words.append(words)
+
+        def load_b_scales(half):
+            for quad in range(4):
+                nc.sync.dma_start(
+                    out=b_planes[half][32 * quad : 32 * quad + 16, :].bitcast(I32),
+                    in_=x8_scales[4 * half : 4 * half + 4, 4 * quad : 4 * quad + 4, :].bitcast(I32),
+                )
+
+        early_cols = EARLY_SCALE_GROUPS * K_PASS
+        as_early = keep.tile([P, DIM_PASSES, early_cols], U8, align_bytes=64)
+        spread_col = SPREAD_FROM * K_PASS
+        as_late = keep.tile([P, DIM_PASSES, spread_col - early_cols], U8, align_bytes=64)
+        as_spread = keep.tile([P, K_PASS], U8, align_bytes=64)
+        as_sorted = keep.tile([P, PACK, P], U8, align_bytes=64)
+        as_plane = keep.tile([P, DIM_PASSES, GROUPS - SPREAD_FROM, PACK, P], U8, align_bytes=64)
+        th_plane = keep.tile([P, DIM_PASSES, CHAINS], U8, align_bytes=64)
+        b_planes = []
+        for half in range(2):
+            plane = keep.tile([P, DIM], U8, name="b_plane%d" % half, align_bytes=64)
+            b_planes.append(plane)
+        warm = keep.tile([P, 2], F32)
+        nc.vector.memset(as_early[:].bitcast(I32), 0)
+        nc.vector.memset(th_plane[:].bitcast(I32), 0)
+        nc.vector.memset(warm[:, 0:1], 0.0)
+        nc.vector.memset(as_late[:].bitcast(I32), 0)
+        nc.vector.memset(as_plane[:].bitcast(I32), 0)
+        for half in range(2):
+            nc.vector.memset(b_planes[half][:].bitcast(I32), 0)
+        nc.scalar.activation(out=warm[:, 1:2], in_=warm[:, 0:1], func=ACT.Sigmoid, scale=-1.0)
+
+        load_a(0)
+        load_scale_rows([nc.sync] * 4, as_early, x4_scales[:, :, 0:early_cols])
+        th_words = keep.tile([P, DIM_PASSES, 2 * CHAINS], U8, align_bytes=64)
+        nc.sync.dma_start(out=th_words[:].bitcast(I32), in_=theta_words.bitcast(I32).rearrange("k p c -> p k c"))
+        load_scale_rows([nc.sync] * 4, th_plane, theta_scales)
+        load_a(1)
+        w_bf = keep.tile([P, GROUPS, PACK], BF16)
+        nc.sync.dma_start(out=w_bf[:], in_=weight.rearrange("(g p t) -> p g t", p=P, t=PACK))
+        load_scale_rows([nc.sync] * 4, as_late, x4_scales[:, :, early_cols:spread_col])
+        nc.sync.dma_start(
+            out=as_spread[:].bitcast(I32),
+            in_=x4_scales[:, :, spread_col:OBS].rearrange("k q (h c) -> (k q) h c", c=K_PASS).bitcast(I32),
+        )
+        load_a(2)
+        load_a(3)
+        load_b_scales(0)
+        load_b(0)
+        load_a(4)
+
+        a_codes = []
+        a_scales = []
+
+        def sort_columns(g):
+            codes = keep.tile([P, DIM_PASSES, PACK, 2 * P], U8, name="a_codes%d" % g, align_bytes=64)
+            nc.vector.tensor_copy(
+                out=codes[:].rearrange("p k t (m b) -> p k t m b", b=2),
+                in_=a_raw[g][:].rearrange("p k (m t b) -> p k t m b", t=PACK, b=2),
+            )
+            a_codes.append(codes)
+            if g >= SPREAD_FROM:
+                a_scales.append(as_plane[:, :, g - SPREAD_FROM, :, :])
+                return
+            if g < EARLY_SCALE_GROUPS:
+                rows = as_early[:, :, g * K_PASS : (g + 1) * K_PASS]
+            else:
+                rows = as_late[:, :, g * K_PASS - early_cols : (g + 1) * K_PASS - early_cols]
+            scales = keep.tile([P, DIM_PASSES, PACK, P], U8, name="a_scales%d" % g, align_bytes=64)
+            nc.vector.tensor_copy(out=scales[:], in_=rows.rearrange("p k (m t) -> p k t m", t=PACK))
+            a_scales.append(scales)
+
+        def margin_bank(i):
+            return i if i < BANKS else EARLY_TILES + (i - BANKS) % (BANKS - EARLY_TILES)
+
+        sig = {}
+
+        def margins(g, t):
+            z = psum.tile([P, CHAINS], F32, name="z", tag="bank%d" % margin_bank(PACK * g + t))
+            for k in range(DIM_PASSES):
+                nc.tensor.matmul_mx(
+                    out=z[:],
+                    lhsT=a_codes[g][:, k, t, :].bitcast(FP4X4),
+                    lhsT_scale=a_scales[g][:, k, t, :],
+                    rhs=th_words[:, k, :].bitcast(FP4X4),
+                    rhs_scale=th_plane[:, k, :],
+                    start=(k == 0),
+                    stop=(k == DIM_PASSES - 1),
+                )
+            s = work.tile([P, CHAINS], F32, name="sig", bufs=6)
+            nc.scalar.activation(out=s[:], in_=z[:], func=ACT.Sigmoid, scale=-1.0)
+            sig[(g, t)] = s
+
+        r_rows = {}
+
+        def weigh(g, t):
+            if g not in r_rows:
+                rows = work.tile([P, PACK, CHAINS], BF16, name="r_rows", bufs=3)
+                r_rows[g] = rows
+            if t >= PACK - SCALAR_MULS[g]:
+                nc.scalar.activation(out=r_rows[g][:, t, :], in_=sig[(g, t)][:], func=ACT.Copy, scale=w_f32[:, g, t : t + 1])
+            else:
+                nc.vector.tensor_scalar(
+                    out=r_rows[g][:, t, :], in0=sig[(g, t)][:], scalar1=w_f32[:, g, t : t + 1], scalar2=None, op0=ALU.mult
+                )
+
+        r_grouped = {}
+        r_codes = {}
+        r_scales = {}
+
+        def interleave(g):
+            grouped = work.tile([P, CHAINS, PACK], BF16, name="r_grouped", bufs=2, align_bytes=64)
+            nc.vector.tensor_copy(out=grouped[:], in_=r_rows[g][:].rearrange("p t c -> p c t"))
+            r_grouped[g] = grouped
+
+        def quantize(g):
+            codes = keep.tile([P, CHAINS], U32, name="r_codes%d" % g, align_bytes=64)
+            scales = keep.tile([P, CHAINS], U8, name="r_scales%d" % g, align_bytes=64)
+            nc.vector.quantize_mx(
+                out=codes[:].bitcast(FP8X4), scales=scales[:], in_=r_grouped[g][:].rearrange("p c t -> p (c t)")
+            )
+            r_codes[g] = codes
+            r_scales[g] = scales
+
+        grad = {}
+
+        pieces = [(j, 0, CHAINS) for j in range(DIM_TILES - 1)]
+        pieces.extend([(DIM_TILES - 1, 0, 256), (DIM_TILES - 1, 256, 384), (DIM_TILES - 1, 384, CHAINS)])
+
+        def gradient(piece, g):
+            j, c0, c1 = piece
+            if g == 0:
+                acc = psum.tile([P, c1 - c0], F32, name="grad", tag="bank%d" % (pieces.index(piece) % BANKS))
+                grad[piece] = acc
+            nc.tensor.matmul_mx(
+                out=grad[piece][:],
+                lhsT=b_words[g][:, P * j : P * (j + 1)].bitcast(FP8X4),
+                lhsT_scale=b_planes[g // 4][4 * (g % 4) : P, P * j : P * (j + 1)],
+                rhs=r_codes[g][:, c0:c1].bitcast(FP8X4),
+                rhs_scale=r_scales[g][:, c0:c1],
+                start=(g == 0),
+                stop=(g == GROUPS - 1),
+            )
+
+        sort_columns(0)
+        sort_columns(1)
+        w_f32 = keep.tile([P, GROUPS, PACK], F32)
+        nc.vector.tensor_copy(out=w_f32[:], in_=w_bf[:])
+        step_all = keep.tile([P, CHAINS], BF16)
+        mom_sb = keep.tile([P, DIM_TILES, CHAINS], BF16)
+
+        def sort_late_scales_and_load_the_rest():
+            nc.vector.tensor_copy(out=as_sorted[:], in_=as_spread[:].rearrange("p (m t) -> p t m", t=PACK))
+            for k in range(DIM_PASSES):
+                for quad in range(4):
+                    first = 64 * k + 16 * quad
+                    nc.sync.dma_start(
+                        out=as_plane[32 * quad : 32 * quad + 4, k, :, :, :].rearrange("r h t m -> r (h t m)").bitcast(I32),
+                        in_=as_sorted[first : first + 16, :, :].rearrange("p t m -> p (t m)").bitcast(I32),
+                    )
+            load_b(1)
+            load_a(5)
+            load_b_scales(1)
+            load_b(2)
+            load_a(6)
+            load_b(3)
+            load_a(7)
+            for g in range(4, GROUPS):
+                load_b(g)
+            nc.sync.dma_start(out=step_all[:], in_=step.partition_broadcast(P))
+            nc.sync.dma_start(out=mom_sb[:], in_=mom.rearrange("(j p) c -> p j c", p=P))
+
+        for g in range(GROUPS):
+            first_scalar = PACK - SCALAR_MULS[g]
+            for t in range(PACK):
+                margins(g, t)
+                if t == 0 and g > 0:
+                    interleave(g - 1)
+                if t < first_scalar:
+                    weigh(g, t)
+                if t - 1 >= first_scalar:
+                    weigh(g, t - 1)
+                if t == 0 and g > 0:
+                    quantize(g - 1)
+                if t == 1 and g + 2 < GROUPS:
+                    sort_columns(g + 2)
+                if t == 1 and g == 0:
+                    sort_late_scales_and_load_the_rest()
+                if t == 2 and 2 <= g < GROUPS - 1:
+                    for j in range(EARLY_TILES):
+                        gradient(pieces[j], g - 2)
+            if PACK - 1 >= first_scalar:
+                weigh(g, PACK - 1)
+        last = GROUPS - 1
+        interleave(last)
+        quantize(last)
+
+        for g in range(last - 2, GROUPS):
+            for j in range(EARLY_TILES):
+                gradient(pieces[j], g)
+
+        scaled = {}
+
+        def scale_gradient(piece):
+            j, c0, c1 = piece
+            tmp = keep.tile([P, c1 - c0], F32, name="scaled%d_%d" % (j, c0))
+            nc.vector.tensor_tensor(out=tmp[:], in0=grad[piece][:], in1=step_all[:, c0:c1], op=ALU.mult)
+            scaled[piece] = tmp
+
+        def kick(piece, engine):
+            j, c0, c1 = piece
+            res = keep.tile([P, c1 - c0], F32, name="res%d_%d" % (j, c0))
+            engine.tensor_tensor(out=res[:], in0=scaled[piece][:], in1=mom_sb[:, j, c0:c1], op=ALU.add)
+            nc.sync.dma_start(out=out[P * j : P * (j + 1), c0:c1], in_=res[:])
+
+        for i in range(EARLY_TILES):
+            scale_gradient(pieces[i])
+            if i < GPSIMD_ADDS:
+                kick(pieces[i], nc.gpsimd)
+        for piece in pieces[EARLY_TILES:]:
+            for g in range(GROUPS):
+                gradient(piece, g)
+        kick(pieces[GPSIMD_ADDS], nc.vector)
+        scale_gradient(pieces[EARLY_TILES])
+        for i in range(GPSIMD_ADDS + 1, EARLY_TILES + 1):
+            kick(pieces[i], nc.vector)
+        scale_gradient(pieces[EARLY_TILES + 1])
+        for i in range(EARLY_TILES + 1, len(pieces) - 1):
+            scale_gradient(pieces[i + 1])
+            kick(pieces[i], nc.vector)
+        kick(pieces[-1], nc.vector)

@@ -24,8 +24,14 @@ DIM_TILES = DIM // P
 BANKS = 8
 EARLY_TILES = 5
 EARLY_SCALE_GROUPS = 2
-SPREAD_FROM = 4
-SCALAR_MULS = [0, 3, 2, 2, 2, 2, 2, 0]
+SPREAD_WIDE = 4
+A_LOADS = [(0, 2), (2, 4), (4, 6), (6, 8)]
+SCALAR_MULS = [[], [2, 3], [1, 2, 3], [2, 3], [1, 2, 3], [2, 3], [3], [0]]
+LAST_SPLIT = 320
+FILL = 4
+M6 = 5
+SORT_FROM = 1
+WOVEN = [1, 1, 2, 1]
 GPSIMD_ADDS = 2
 
 
@@ -49,13 +55,14 @@ def tile_hmc_logistic_kick_s4_kernel(
         a_words_i32 = x4_words.bitcast(I32)
         a_raw = []
 
-        def load_a(g):
-            raw = keep.tile([P, DIM_PASSES, 2 * K_PASS], U8, name="a_raw%d" % g, align_bytes=64)
+        def load_a(first, stop):
+            raw = keep.tile([P, DIM_PASSES, (stop - first) * 2 * K_PASS], U8, name="a_raw%d" % first, align_bytes=64)
             nc.sync.dma_start(
                 out=raw[:].bitcast(I32),
-                in_=a_words_i32[:, :, 256 * g : 256 * (g + 1)].rearrange("k p c -> p k c"),
+                in_=a_words_i32[:, :, 256 * first : 256 * stop].rearrange("k p c -> p k c"),
             )
-            a_raw.append(raw)
+            for i in range(stop - first):
+                a_raw.append(raw[:, :, 2 * K_PASS * i : 2 * K_PASS * (i + 1)])
 
         b_words = []
 
@@ -76,44 +83,39 @@ def tile_hmc_logistic_kick_s4_kernel(
 
         early_cols = EARLY_SCALE_GROUPS * K_PASS
         as_early = keep.tile([P, DIM_PASSES, early_cols], U8, align_bytes=64)
-        spread_col = SPREAD_FROM * K_PASS
-        as_late = keep.tile([P, DIM_PASSES, spread_col - early_cols], U8, align_bytes=64)
-        as_spread = keep.tile([P, K_PASS], U8, align_bytes=64)
-        as_sorted = keep.tile([P, PACK, P], U8, align_bytes=64)
-        as_plane = keep.tile([P, DIM_PASSES, GROUPS - SPREAD_FROM, PACK, P], U8, align_bytes=64)
+        wide_stop = early_cols + SPREAD_WIDE * K_PASS
+        as_spread = keep.tile([P, 2, K_PASS], U8, name="as_spread", align_bytes=64)
+        as_sorted = keep.tile([P, 2, PACK, P], U8, name="as_sorted", align_bytes=64)
+        as_plane = keep.tile([P, DIM_PASSES, GROUPS - EARLY_SCALE_GROUPS, PACK, P], U8, name="as_plane", align_bytes=64)
         th_plane = keep.tile([P, DIM_PASSES, CHAINS], U8, align_bytes=64)
         b_planes = []
         for half in range(2):
             plane = keep.tile([P, DIM], U8, name="b_plane%d" % half, align_bytes=64)
             b_planes.append(plane)
-        warm = keep.tile([P, 2], F32)
-        nc.vector.memset(as_early[:].bitcast(I32), 0)
+        nc.gpsimd.memset(as_early[:].bitcast(I32), 0)
         nc.vector.memset(th_plane[:].bitcast(I32), 0)
-        nc.vector.memset(warm[:, 0:1], 0.0)
-        nc.vector.memset(as_late[:].bitcast(I32), 0)
+        nc.vector.memset(as_spread[:, 1, :].bitcast(I32), 0)
         nc.vector.memset(as_plane[:].bitcast(I32), 0)
         for half in range(2):
             nc.vector.memset(b_planes[half][:].bitcast(I32), 0)
-        nc.scalar.activation(out=warm[:, 1:2], in_=warm[:, 0:1], func=ACT.Sigmoid, scale=-1.0)
 
-        load_a(0)
+        load_a(*A_LOADS[0])
         load_scale_rows([nc.sync] * 4, as_early, x4_scales[:, :, 0:early_cols])
         th_words = keep.tile([P, DIM_PASSES, 2 * CHAINS], U8, align_bytes=64)
         nc.sync.dma_start(out=th_words[:].bitcast(I32), in_=theta_words.bitcast(I32).rearrange("k p c -> p k c"))
         load_scale_rows([nc.sync] * 4, th_plane, theta_scales)
-        load_a(1)
-        w_bf = keep.tile([P, GROUPS, PACK], BF16)
-        nc.sync.dma_start(out=w_bf[:], in_=weight.rearrange("(g p t) -> p g t", p=P, t=PACK))
-        load_scale_rows([nc.sync] * 4, as_late, x4_scales[:, :, early_cols:spread_col])
         nc.sync.dma_start(
-            out=as_spread[:].bitcast(I32),
-            in_=x4_scales[:, :, spread_col:OBS].rearrange("k q (h c) -> (k q) h c", c=K_PASS).bitcast(I32),
+            out=as_spread[:, 0, :].bitcast(I32),
+            in_=x4_scales[:, :, early_cols:wide_stop].rearrange("k q (h c) -> (k q) h c", c=K_PASS).bitcast(I32),
         )
-        load_a(2)
-        load_a(3)
-        load_b_scales(0)
+        nc.sync.dma_start(
+            out=as_spread[0:64, 1, :].bitcast(I32),
+            in_=x4_scales[:, :, wide_stop:OBS].rearrange("k q (h c) -> (k q) h c", c=K_PASS).bitcast(I32),
+        )
+        w_bf = keep.tile([P, GROUPS, PACK], BF16, name="w_bf")
+        nc.sync.dma_start(out=w_bf[:], in_=weight.rearrange("(g p t) -> p g t", p=P, t=PACK))
+        load_a(*A_LOADS[1])
         load_b(0)
-        load_a(4)
 
         a_codes = []
         a_scales = []
@@ -122,16 +124,13 @@ def tile_hmc_logistic_kick_s4_kernel(
             codes = keep.tile([P, DIM_PASSES, PACK, 2 * P], U8, name="a_codes%d" % g, align_bytes=64)
             nc.vector.tensor_copy(
                 out=codes[:].rearrange("p k t (m b) -> p k t m b", b=2),
-                in_=a_raw[g][:].rearrange("p k (m t b) -> p k t m b", t=PACK, b=2),
+                in_=a_raw[g].rearrange("p k (m t b) -> p k t m b", t=PACK, b=2),
             )
             a_codes.append(codes)
-            if g >= SPREAD_FROM:
-                a_scales.append(as_plane[:, :, g - SPREAD_FROM, :, :])
+            if g >= EARLY_SCALE_GROUPS:
+                a_scales.append(as_plane[:, :, g - EARLY_SCALE_GROUPS, :, :])
                 return
-            if g < EARLY_SCALE_GROUPS:
-                rows = as_early[:, :, g * K_PASS : (g + 1) * K_PASS]
-            else:
-                rows = as_late[:, :, g * K_PASS - early_cols : (g + 1) * K_PASS - early_cols]
+            rows = as_early[:, :, g * K_PASS : (g + 1) * K_PASS]
             scales = keep.tile([P, DIM_PASSES, PACK, P], U8, name="a_scales%d" % g, align_bytes=64)
             nc.vector.tensor_copy(out=scales[:], in_=rows.rearrange("p k (m t) -> p k t m", t=PACK))
             a_scales.append(scales)
@@ -163,7 +162,7 @@ def tile_hmc_logistic_kick_s4_kernel(
             if g not in r_rows:
                 rows = work.tile([P, PACK, CHAINS], BF16, name="r_rows", bufs=3)
                 r_rows[g] = rows
-            if t >= PACK - SCALAR_MULS[g]:
+            if t in SCALAR_MULS[g]:
                 nc.scalar.activation(out=r_rows[g][:, t, :], in_=sig[(g, t)][:], func=ACT.Copy, scale=w_f32[:, g, t : t + 1])
             else:
                 nc.vector.tensor_scalar(
@@ -176,7 +175,16 @@ def tile_hmc_logistic_kick_s4_kernel(
 
         def interleave(g):
             grouped = work.tile([P, CHAINS, PACK], BF16, name="r_grouped", bufs=2, align_bytes=64)
-            nc.vector.tensor_copy(out=grouped[:], in_=r_rows[g][:].rearrange("p t c -> p c t"))
+            split = LAST_SPLIT if g == GROUPS - 1 else CHAINS
+            nc.vector.tensor_copy(
+                out=grouped[:, 0:split, :].rearrange("p (c i) t -> p c t i", i=4),
+                in_=r_rows[g][:, :, 0:split].rearrange("p t (c i) -> p c t i", i=4),
+            )
+            if split < CHAINS:
+                nc.scalar.copy(
+                    out=grouped[:, split:CHAINS, :].rearrange("p (c i) t -> p c t i", i=4),
+                    in_=r_rows[g][:, :, split:CHAINS].rearrange("p t (c i) -> p c t i", i=4),
+                )
             r_grouped[g] = grouped
 
         def quantize(g):
@@ -208,62 +216,75 @@ def tile_hmc_logistic_kick_s4_kernel(
                 stop=(g == GROUPS - 1),
             )
 
-        sort_columns(0)
-        sort_columns(1)
-        w_f32 = keep.tile([P, GROUPS, PACK], F32)
-        nc.vector.tensor_copy(out=w_f32[:], in_=w_bf[:])
-        step_all = keep.tile([P, CHAINS], BF16)
-        mom_sb = keep.tile([P, DIM_TILES, CHAINS], BF16)
-
-        def sort_late_scales_and_load_the_rest():
-            nc.vector.tensor_copy(out=as_sorted[:], in_=as_spread[:].rearrange("p (m t) -> p t m", t=PACK))
+        def place_scales(slot, first, count):
             for k in range(DIM_PASSES):
                 for quad in range(4):
-                    first = 64 * k + 16 * quad
+                    row = count * (16 * k + 4 * quad)
                     nc.sync.dma_start(
-                        out=as_plane[32 * quad : 32 * quad + 4, k, :, :, :].rearrange("r h t m -> r (h t m)").bitcast(I32),
-                        in_=as_sorted[first : first + 16, :, :].rearrange("p t m -> p (t m)").bitcast(I32),
+                        out=as_plane[32 * quad : 32 * quad + 4, k, first : first + count, :, :]
+                        .rearrange("r h t m -> r (h t m)")
+                        .bitcast(I32),
+                        in_=as_sorted[row : row + 4 * count, slot, :, :].rearrange("p t m -> p (t m)").bitcast(I32),
                     )
-            load_b(1)
-            load_a(5)
-            load_b_scales(1)
-            load_b(2)
-            load_a(6)
-            load_b(3)
-            load_a(7)
-            for g in range(4, GROUPS):
-                load_b(g)
-            nc.sync.dma_start(out=step_all[:], in_=step.partition_broadcast(P))
-            nc.sync.dma_start(out=mom_sb[:], in_=mom.rearrange("(j p) c -> p j c", p=P))
+
+        sort_columns(0)
+        sort_columns(1)
+        nc.vector.tensor_copy(out=as_sorted[:], in_=as_spread[:].rearrange("p s (m t) -> p s t m", t=PACK))
+        w_f32 = keep.tile([P, GROUPS, PACK], F32, name="w_f32")
+        nc.vector.tensor_copy(out=w_f32[:], in_=w_bf[:])
+        sort_columns(2)
+        place_scales(0, 0, SPREAD_WIDE)
+        load_b_scales(0)
+        load_a(*A_LOADS[2])
+        load_b(1)
+        place_scales(1, SPREAD_WIDE, GROUPS - EARLY_SCALE_GROUPS - SPREAD_WIDE)
+        load_b(2)
+        load_a(*A_LOADS[3])
+        load_b_scales(1)
+        for g in range(3, GROUPS):
+            load_b(g)
+        step_all = keep.tile([P, CHAINS], BF16, name="step_all")
+        nc.sync.dma_start(out=step_all[:], in_=step.partition_broadcast(P))
+        mom_sb = keep.tile([P, DIM_TILES, CHAINS], BF16, name="mom_sb")
+        nc.sync.dma_start(out=mom_sb[:], in_=mom.rearrange("(j p) c -> p j c", p=P))
+
+        todo = [(j, g) for g in range(GROUPS) for j in range(EARLY_TILES)]
+
+        def early_pass():
+            j, g = todo[0]
+            todo.remove((j, g))
+            gradient(pieces[j], g)
 
         for g in range(GROUPS):
-            first_scalar = PACK - SCALAR_MULS[g]
             for t in range(PACK):
                 margins(g, t)
                 if t == 0 and g > 0:
                     interleave(g - 1)
-                if t < first_scalar:
+                if t not in SCALAR_MULS[g]:
                     weigh(g, t)
-                if t - 1 >= first_scalar:
+                if t - 1 in SCALAR_MULS[g]:
                     weigh(g, t - 1)
-                if t == 0 and g > 0:
+                if t == min(u for u in range(PACK) if u not in SCALAR_MULS[g]) and g > 0:
                     quantize(g - 1)
-                if t == 1 and g + 2 < GROUPS:
-                    sort_columns(g + 2)
-                if t == 1 and g == 0:
-                    sort_late_scales_and_load_the_rest()
-                if t == 2 and 2 <= g < GROUPS - 1:
-                    for j in range(EARLY_TILES):
-                        gradient(pieces[j], g - 2)
-            if PACK - 1 >= first_scalar:
+                if t == 1 and len(a_codes) < GROUPS and g >= SORT_FROM:
+                    sort_columns(len(a_codes))
+                if (g, t) >= (2, 2):
+                    for rep in range(WOVEN[t]):
+                        early_pass()
+            if PACK - 1 in SCALAR_MULS[g]:
                 weigh(g, PACK - 1)
         last = GROUPS - 1
         interleave(last)
         quantize(last)
 
-        for g in range(last - 2, GROUPS):
-            for j in range(EARLY_TILES):
-                gradient(pieces[j], g)
+        for rep in range(len(todo) - EARLY_TILES):
+            early_pass()
+        for g in range(FILL):
+            gradient(pieces[EARLY_TILES], g)
+        for j in range(EARLY_TILES):
+            gradient(pieces[j], last)
+        for g in range(FILL, GROUPS):
+            gradient(pieces[EARLY_TILES], g)
 
         scaled = {}
 
@@ -283,14 +304,14 @@ def tile_hmc_logistic_kick_s4_kernel(
             scale_gradient(pieces[i])
             if i < GPSIMD_ADDS:
                 kick(pieces[i], nc.gpsimd)
-        for piece in pieces[EARLY_TILES:]:
+        for piece in pieces[EARLY_TILES + 1 :]:
             for g in range(GROUPS):
                 gradient(piece, g)
-        kick(pieces[GPSIMD_ADDS], nc.vector)
         scale_gradient(pieces[EARLY_TILES])
-        for i in range(GPSIMD_ADDS + 1, EARLY_TILES + 1):
+        for i in range(GPSIMD_ADDS, EARLY_TILES + 1):
+            if i == M6:
+                scale_gradient(pieces[EARLY_TILES + 1])
             kick(pieces[i], nc.vector)
-        scale_gradient(pieces[EARLY_TILES + 1])
         for i in range(EARLY_TILES + 1, len(pieces) - 1):
             scale_gradient(pieces[i + 1])
             kick(pieces[i], nc.vector)

@@ -29,6 +29,8 @@ A_LOADS = [(0, 2), (2, 4), (4, 6), (6, 8)]
 SCALAR_MULS = [[], [2, 3], [1, 2, 3], [2, 3], [1, 2, 3], [2, 3], [3], [0]]
 LAST_SPLIT = 320
 FILL = 4
+WARM_PASSES = 3
+SPLIT0 = 4
 M6 = 5
 SORT_FROM = 1
 WOVEN = [1, 1, 2, 1]
@@ -122,10 +124,10 @@ def tile_hmc_logistic_kick_s4_kernel(
 
         def sort_columns(g):
             codes = keep.tile([P, DIM_PASSES, PACK, 2 * P], U8, name="a_codes%d" % g, align_bytes=64)
-            nc.vector.tensor_copy(
-                out=codes[:].rearrange("p k t (m b) -> p k t m b", b=2),
-                in_=a_raw[g].rearrange("p k (m t b) -> p k t m b", t=PACK, b=2),
-            )
+            sorted_view = codes[:].rearrange("p k t (m b) -> p k t m b", b=2)
+            raw_view = a_raw[g].rearrange("p k (m t b) -> p k t m b", t=PACK, b=2)
+            ahead = SPLIT0 if g == 0 else PACK
+            nc.vector.tensor_copy(out=sorted_view[:, :, 0:ahead], in_=raw_view[:, :, 0:ahead])
             a_codes.append(codes)
             if g >= EARLY_SCALE_GROUPS:
                 a_scales.append(as_plane[:, :, g - EARLY_SCALE_GROUPS, :, :])
@@ -134,6 +136,8 @@ def tile_hmc_logistic_kick_s4_kernel(
             scales = keep.tile([P, DIM_PASSES, PACK, P], U8, name="a_scales%d" % g, align_bytes=64)
             nc.vector.tensor_copy(out=scales[:], in_=rows.rearrange("p k (m t) -> p k t m", t=PACK))
             a_scales.append(scales)
+            if ahead < PACK:
+                nc.vector.tensor_copy(out=sorted_view[:, :, ahead:PACK], in_=raw_view[:, :, ahead:PACK])
 
         def margin_bank(i):
             return i if i < BANKS else EARLY_TILES + (i - BANKS) % (BANKS - EARLY_TILES)
@@ -227,6 +231,17 @@ def tile_hmc_logistic_kick_s4_kernel(
                         in_=as_sorted[row : row + 4 * count, slot, :, :].rearrange("p t m -> p (t m)").bitcast(I32),
                     )
 
+        warm = psum.tile([P, CHAINS], F32, name="warm", tag="bank%d" % (BANKS - 1))
+        for rep in range(WARM_PASSES):
+            nc.tensor.matmul_mx(
+                out=warm[:],
+                lhsT=a_raw[0][:, 0, 0 : 2 * P].bitcast(FP4X4),
+                lhsT_scale=as_early[:, 0, 0:P],
+                rhs=a_raw[0][:, 0, :].bitcast(FP4X4),
+                rhs_scale=as_early[:, 0, 0:K_PASS],
+                start=(rep == 0),
+                stop=(rep == WARM_PASSES - 1),
+            )
         sort_columns(0)
         sort_columns(1)
         nc.vector.tensor_copy(out=as_sorted[:], in_=as_spread[:].rearrange("p s (m t) -> p s t m", t=PACK))

@@ -16,25 +16,32 @@ ACT = mybir.ActivationFunctionType
 ALU = mybir.AluOpType
 
 P = 128
-PACK = 4
-K_PASS = P * PACK
+QUADS = 4
+SLOTS = 4
+K_PASS = P * SLOTS
 GROUPS = OBS // K_PASS
 DIM_PASSES = DIM // K_PASS
 DIM_TILES = DIM // P
 BANKS = 8
+FP4_BYTES = 2
+
 EARLY_TILES = 5
-EARLY_SCALE_GROUPS = 2
-SPREAD_WIDE = 4
-A_LOADS = [(0, 2), (2, 4), (4, 6), (6, 8)]
-SCALAR_MULS = [[], [2, 3], [1, 2, 3], [2, 3], [1, 2, 3], [2, 3], [3], [0]]
-LAST_SPLIT = 320
-FILL = 4
+EXTRA_PASS_SLOT = 2
+DIRECT_GROUPS = 2
+SPREAD_RUNS = [(2, 4), (6, 2)]
+LAST_VECTOR_CHAINS = 320
+FILL_PASSES = 4
+GPSIMD_SUMS = 2
+LAST_TILE_CUTS = [0, 256, 384, CHAINS]
 WARM_PASSES = 3
-SPLIT0 = 4
-M6 = 5
-SORT_FROM = 1
-WOVEN = [1, 1, 2, 1]
-GPSIMD_ADDS = 2
+
+
+def scalar_slots(g):
+    if g == 0:
+        return []
+    if g + 2 < GROUPS:
+        return list(range(1 + g % 2, SLOTS))
+    return [0]
 
 
 def tile_hmc_logistic_kick_s4_kernel(
@@ -47,139 +54,153 @@ def tile_hmc_logistic_kick_s4_kernel(
         psum = ctx.enter_context(tc.psum_pool(name="psum", bufs=1))
         ctx.enter_context(tc.manual_schedule())
 
-        def load_scale_rows(queues, plane, rows):
-            for quad in range(4):
-                queues[quad].dma_start(
+        a_direct = keep.tile([P, DIM_PASSES, DIRECT_GROUPS * K_PASS], U8, align_bytes=64)
+        theta_plane = keep.tile([P, DIM_PASSES, CHAINS], U8, align_bytes=64)
+        spread_raw, spread_sorted, spread_plane = [], [], []
+        for first, count in SPREAD_RUNS:
+            raw_rows = keep.tile([P, K_PASS], U8, name="spread_raw%d" % first, align_bytes=64)
+            sorted_rows = keep.tile([P, SLOTS, P], U8, name="spread_sorted%d" % first, align_bytes=64)
+            run_plane = keep.tile([P, count, DIM_PASSES, SLOTS, P], U8, name="spread_plane%d" % first, align_bytes=64)
+            spread_raw.append(raw_rows)
+            spread_sorted.append(sorted_rows)
+            spread_plane.append(run_plane)
+        b_planes = []
+        for half in range(GROUPS // 4):
+            packed = keep.tile([P, DIM], U8, name="b_planes%d" % half, align_bytes=64)
+            b_planes.append(packed)
+        nc.gpsimd.memset(a_direct[:].bitcast(I32), 0)
+        nc.vector.memset(theta_plane[:].bitcast(I32), 0)
+        for run_plane in spread_plane:
+            nc.vector.memset(run_plane[:].bitcast(I32), 0)
+        nc.vector.memset(spread_raw[1][:].bitcast(I32), 0)
+        for packed in b_planes:
+            nc.vector.memset(packed[:].bitcast(I32), 0)
+
+        a_raw = []
+        b_words = []
+        group_bytes = FP4_BYTES * K_PASS
+
+        def load_a(first, stop):
+            raw = keep.tile([P, DIM_PASSES, (stop - first) * group_bytes], U8, name="a_raw%d" % first, align_bytes=64)
+            nc.sync.dma_start(
+                out=raw[:].bitcast(I32),
+                in_=x4_words[:, :, first * group_bytes : stop * group_bytes].rearrange("k p c -> p k c").bitcast(I32),
+            )
+            for i in range(stop - first):
+                a_raw.append(raw[:, :, i * group_bytes : (i + 1) * group_bytes])
+
+        def load_scale_rows(plane, rows, quads):
+            for quad in quads:
+                nc.sync.dma_start(
                     out=plane[32 * quad : 32 * quad + 4, :, :].bitcast(I32),
                     in_=rows[:, 4 * quad : 4 * quad + 4, :].rearrange("k r c -> r k c").bitcast(I32),
                 )
 
-        a_words_i32 = x4_words.bitcast(I32)
-        a_raw = []
-
-        def load_a(first, stop):
-            raw = keep.tile([P, DIM_PASSES, (stop - first) * 2 * K_PASS], U8, name="a_raw%d" % first, align_bytes=64)
-            nc.sync.dma_start(
-                out=raw[:].bitcast(I32),
-                in_=a_words_i32[:, :, 256 * first : 256 * stop].rearrange("k p c -> p k c"),
-            )
-            for i in range(stop - first):
-                a_raw.append(raw[:, :, 2 * K_PASS * i : 2 * K_PASS * (i + 1)])
-
-        b_words = []
+        def load_spread(run):
+            first, count = SPREAD_RUNS[run]
+            for k in range(DIM_PASSES):
+                nc.sync.dma_start(
+                    out=spread_raw[run][k : 32 * count : DIM_PASSES, :].bitcast(I32),
+                    in_=x4_scales[k, :, first * K_PASS : (first + count) * K_PASS]
+                    .rearrange("q (h c) -> q h c", c=K_PASS)
+                    .bitcast(I32),
+                )
 
         def load_b(g):
             words = keep.tile([P, DIM], U32, name="b_words%d" % g, align_bytes=64)
-            nc.sync.dma_start(
-                out=words[:].bitcast(I32),
-                in_=x8_words[g].rearrange("p n t -> p (n t)").bitcast(I32),
-            )
+            nc.sync.dma_start(out=words[:].bitcast(I32), in_=x8_words[g].rearrange("p n t -> p (n t)").bitcast(I32))
             b_words.append(words)
 
         def load_b_scales(half):
-            for quad in range(4):
+            for quad in range(QUADS):
                 nc.sync.dma_start(
                     out=b_planes[half][32 * quad : 32 * quad + 16, :].bitcast(I32),
                     in_=x8_scales[4 * half : 4 * half + 4, 4 * quad : 4 * quad + 4, :].bitcast(I32),
                 )
 
-        early_cols = EARLY_SCALE_GROUPS * K_PASS
-        as_early = keep.tile([P, DIM_PASSES, early_cols], U8, align_bytes=64)
-        wide_stop = early_cols + SPREAD_WIDE * K_PASS
-        as_spread = keep.tile([P, 2, K_PASS], U8, name="as_spread", align_bytes=64)
-        as_sorted = keep.tile([P, 2, PACK, P], U8, name="as_sorted", align_bytes=64)
-        as_plane = keep.tile([P, DIM_PASSES, GROUPS - EARLY_SCALE_GROUPS, PACK, P], U8, name="as_plane", align_bytes=64)
-        th_plane = keep.tile([P, DIM_PASSES, CHAINS], U8, align_bytes=64)
-        b_planes = []
-        for half in range(2):
-            plane = keep.tile([P, DIM], U8, name="b_plane%d" % half, align_bytes=64)
-            b_planes.append(plane)
-        nc.gpsimd.memset(as_early[:].bitcast(I32), 0)
-        nc.vector.memset(th_plane[:].bitcast(I32), 0)
-        nc.vector.memset(as_spread[:, 1, :].bitcast(I32), 0)
-        nc.vector.memset(as_plane[:].bitcast(I32), 0)
-        for half in range(2):
-            nc.vector.memset(b_planes[half][:].bitcast(I32), 0)
-
-        load_a(*A_LOADS[0])
-        load_scale_rows([nc.sync] * 4, as_early, x4_scales[:, :, 0:early_cols])
-        th_words = keep.tile([P, DIM_PASSES, 2 * CHAINS], U8, align_bytes=64)
-        nc.sync.dma_start(out=th_words[:].bitcast(I32), in_=theta_words.bitcast(I32).rearrange("k p c -> p k c"))
-        load_scale_rows([nc.sync] * 4, th_plane, theta_scales)
-        nc.sync.dma_start(
-            out=as_spread[:, 0, :].bitcast(I32),
-            in_=x4_scales[:, :, early_cols:wide_stop].rearrange("k q (h c) -> (k q) h c", c=K_PASS).bitcast(I32),
-        )
-        nc.sync.dma_start(
-            out=as_spread[0:64, 1, :].bitcast(I32),
-            in_=x4_scales[:, :, wide_stop:OBS].rearrange("k q (h c) -> (k q) h c", c=K_PASS).bitcast(I32),
-        )
-        w_bf = keep.tile([P, GROUPS, PACK], BF16, name="w_bf")
-        nc.sync.dma_start(out=w_bf[:], in_=weight.rearrange("(g p t) -> p g t", p=P, t=PACK))
-        load_a(*A_LOADS[1])
+        load_a(0, 1)
+        load_scale_rows(a_direct, x4_scales[:, :, 0 : DIRECT_GROUPS * K_PASS], range(QUADS))
+        load_a(1, 3)
+        load_scale_rows(theta_plane, theta_scales, range(QUADS // 2))
+        theta = keep.tile([P, DIM_PASSES, FP4_BYTES * CHAINS], U8, align_bytes=64)
+        nc.sync.dma_start(out=theta[:].bitcast(I32), in_=theta_words.rearrange("k p c -> p k c").bitcast(I32))
+        load_scale_rows(theta_plane, theta_scales, range(QUADS // 2, QUADS))
+        load_spread(0)
+        weight_bf = keep.tile([P, GROUPS, SLOTS], BF16)
+        nc.sync.dma_start(out=weight_bf[:], in_=weight.rearrange("(g p t) -> p g t", p=P, t=SLOTS))
         load_b(0)
+        load_a(3, 5)
 
         a_codes = []
         a_scales = []
 
-        def sort_columns(g):
-            codes = keep.tile([P, DIM_PASSES, PACK, 2 * P], U8, name="a_codes%d" % g, align_bytes=64)
-            sorted_view = codes[:].rearrange("p k t (m b) -> p k t m b", b=2)
-            raw_view = a_raw[g].rearrange("p k (m t b) -> p k t m b", t=PACK, b=2)
-            ahead = SPLIT0 if g == 0 else PACK
-            nc.vector.tensor_copy(out=sorted_view[:, :, 0:ahead], in_=raw_view[:, :, 0:ahead])
+        def sort_group():
+            g = len(a_codes)
+            codes = keep.tile([P, DIM_PASSES, SLOTS, FP4_BYTES * P], U8, name="a_codes%d" % g, align_bytes=64)
+            nc.vector.tensor_copy(
+                out=codes[:].rearrange("p k t (m b) -> p k t m b", b=FP4_BYTES),
+                in_=a_raw[g].rearrange("p k (m t b) -> p k t m b", t=SLOTS, b=FP4_BYTES),
+            )
             a_codes.append(codes)
-            if g >= EARLY_SCALE_GROUPS:
-                a_scales.append(as_plane[:, :, g - EARLY_SCALE_GROUPS, :, :])
-                return
-            rows = as_early[:, :, g * K_PASS : (g + 1) * K_PASS]
-            scales = keep.tile([P, DIM_PASSES, PACK, P], U8, name="a_scales%d" % g, align_bytes=64)
-            nc.vector.tensor_copy(out=scales[:], in_=rows.rearrange("p k (m t) -> p k t m", t=PACK))
-            a_scales.append(scales)
-            if ahead < PACK:
-                nc.vector.tensor_copy(out=sorted_view[:, :, ahead:PACK], in_=raw_view[:, :, ahead:PACK])
+            if g < DIRECT_GROUPS:
+                scales = keep.tile([P, DIM_PASSES, SLOTS, P], U8, name="a_scales%d" % g, align_bytes=64)
+                rows = a_direct[:, :, g * K_PASS : (g + 1) * K_PASS]
+                nc.vector.tensor_copy(out=scales[:], in_=rows.rearrange("p k (m t) -> p k t m", t=SLOTS))
+                a_scales.append(scales)
 
-        def margin_bank(i):
-            return i if i < BANKS else EARLY_TILES + (i - BANKS) % (BANKS - EARLY_TILES)
+        def sort_spread(run):
+            count = SPREAD_RUNS[run][1]
+            nc.vector.tensor_copy(
+                out=spread_sorted[run][:], in_=spread_raw[run][:].rearrange("p (m t) -> p t m", t=SLOTS)
+            )
+            rows = 4 * count * DIM_PASSES
+            for quad in range(QUADS):
+                nc.sync.dma_start(
+                    out=spread_plane[run][32 * quad : 32 * quad + 4].rearrange("r h k t m -> r (h k t m)").bitcast(I32),
+                    in_=spread_sorted[run][rows * quad : rows * (quad + 1)].rearrange("p t m -> p (t m)").bitcast(I32),
+                )
+            for h in range(count):
+                a_scales.append(spread_plane[run][:, h, :, :, :])
 
-        sig = {}
+        sigmoids = {}
+        r_rows = {}
+        r_grouped = {}
+        r_codes = []
+        r_planes = []
 
-        def margins(g, t):
-            z = psum.tile([P, CHAINS], F32, name="z", tag="bank%d" % margin_bank(PACK * g + t))
+        def margin_tile(g, t):
+            i = SLOTS * g + t
+            bank = i if i < BANKS else EARLY_TILES + (i - BANKS) % (BANKS - EARLY_TILES)
+            z = psum.tile([P, CHAINS], F32, name="z", tag="bank%d" % bank)
             for k in range(DIM_PASSES):
                 nc.tensor.matmul_mx(
                     out=z[:],
                     lhsT=a_codes[g][:, k, t, :].bitcast(FP4X4),
                     lhsT_scale=a_scales[g][:, k, t, :],
-                    rhs=th_words[:, k, :].bitcast(FP4X4),
-                    rhs_scale=th_plane[:, k, :],
+                    rhs=theta[:, k, :].bitcast(FP4X4),
+                    rhs_scale=theta_plane[:, k, :],
                     start=(k == 0),
                     stop=(k == DIM_PASSES - 1),
                 )
-            s = work.tile([P, CHAINS], F32, name="sig", bufs=6)
-            nc.scalar.activation(out=s[:], in_=z[:], func=ACT.Sigmoid, scale=-1.0)
-            sig[(g, t)] = s
-
-        r_rows = {}
+            sig = work.tile([P, CHAINS], F32, name="sig", bufs=6)
+            nc.scalar.activation(out=sig[:], in_=z[:], func=ACT.Sigmoid, scale=-1.0)
+            sigmoids[(g, t)] = sig
 
         def weigh(g, t):
             if g not in r_rows:
-                rows = work.tile([P, PACK, CHAINS], BF16, name="r_rows", bufs=3)
+                rows = work.tile([P, SLOTS, CHAINS], BF16, name="r_rows", bufs=3)
                 r_rows[g] = rows
-            if t in SCALAR_MULS[g]:
-                nc.scalar.activation(out=r_rows[g][:, t, :], in_=sig[(g, t)][:], func=ACT.Copy, scale=w_f32[:, g, t : t + 1])
+            factor = weight_f32[:, g, t : t + 1]
+            if t in scalar_slots(g):
+                nc.scalar.activation(out=r_rows[g][:, t, :], in_=sigmoids[(g, t)][:], func=ACT.Copy, scale=factor)
             else:
                 nc.vector.tensor_scalar(
-                    out=r_rows[g][:, t, :], in0=sig[(g, t)][:], scalar1=w_f32[:, g, t : t + 1], scalar2=None, op0=ALU.mult
+                    out=r_rows[g][:, t, :], in0=sigmoids[(g, t)][:], scalar1=factor, scalar2=None, op0=ALU.mult
                 )
 
-        r_grouped = {}
-        r_codes = {}
-        r_scales = {}
-
         def interleave(g):
-            grouped = work.tile([P, CHAINS, PACK], BF16, name="r_grouped", bufs=2, align_bytes=64)
-            split = LAST_SPLIT if g == GROUPS - 1 else CHAINS
+            grouped = work.tile([P, CHAINS, SLOTS], BF16, name="r_grouped", bufs=2, align_bytes=64)
+            split = LAST_VECTOR_CHAINS if g == GROUPS - 1 else CHAINS
             nc.vector.tensor_copy(
                 out=grouped[:, 0:split, :].rearrange("p (c i) t -> p c t i", i=4),
                 in_=r_rows[g][:, :, 0:split].rearrange("p t (c i) -> p c t i", i=4),
@@ -193,141 +214,137 @@ def tile_hmc_logistic_kick_s4_kernel(
 
         def quantize(g):
             codes = keep.tile([P, CHAINS], U32, name="r_codes%d" % g, align_bytes=64)
-            scales = keep.tile([P, CHAINS], U8, name="r_scales%d" % g, align_bytes=64)
+            plane = keep.tile([P, CHAINS], U8, name="r_plane%d" % g, align_bytes=64)
             nc.vector.quantize_mx(
-                out=codes[:].bitcast(FP8X4), scales=scales[:], in_=r_grouped[g][:].rearrange("p c t -> p (c t)")
+                out=codes[:].bitcast(FP8X4), scales=plane[:], in_=r_grouped[g][:].rearrange("p c t -> p (c t)")
             )
-            r_codes[g] = codes
-            r_scales[g] = scales
-
-        grad = {}
+            r_codes.append(codes)
+            r_planes.append(plane)
 
         pieces = [(j, 0, CHAINS) for j in range(DIM_TILES - 1)]
-        pieces.extend([(DIM_TILES - 1, 0, 256), (DIM_TILES - 1, 256, 384), (DIM_TILES - 1, 384, CHAINS)])
+        for i in range(len(LAST_TILE_CUTS) - 1):
+            pieces.append((DIM_TILES - 1, LAST_TILE_CUTS[i], LAST_TILE_CUTS[i + 1]))
+        grad = {}
+        scaled = {}
 
-        def gradient(piece, g):
-            j, c0, c1 = piece
+        def gradient_pass(n, g):
+            j, c0, c1 = pieces[n]
             if g == 0:
-                acc = psum.tile([P, c1 - c0], F32, name="grad", tag="bank%d" % (pieces.index(piece) % BANKS))
-                grad[piece] = acc
+                acc = psum.tile([P, c1 - c0], F32, name="grad", tag="bank%d" % (n % BANKS))
+                grad[n] = acc
             nc.tensor.matmul_mx(
-                out=grad[piece][:],
+                out=grad[n][:],
                 lhsT=b_words[g][:, P * j : P * (j + 1)].bitcast(FP8X4),
                 lhsT_scale=b_planes[g // 4][4 * (g % 4) : P, P * j : P * (j + 1)],
                 rhs=r_codes[g][:, c0:c1].bitcast(FP8X4),
-                rhs_scale=r_scales[g][:, c0:c1],
+                rhs_scale=r_planes[g][:, c0:c1],
                 start=(g == 0),
                 stop=(g == GROUPS - 1),
             )
 
-        def place_scales(slot, first, count):
-            for k in range(DIM_PASSES):
-                for quad in range(4):
-                    row = count * (16 * k + 4 * quad)
-                    nc.sync.dma_start(
-                        out=as_plane[32 * quad : 32 * quad + 4, k, first : first + count, :, :]
-                        .rearrange("r h t m -> r (h t m)")
-                        .bitcast(I32),
-                        in_=as_sorted[row : row + 4 * count, slot, :, :].rearrange("p t m -> p (t m)").bitcast(I32),
-                    )
+        def times_step(n):
+            j, c0, c1 = pieces[n]
+            product = keep.tile([P, c1 - c0], F32, name="scaled%d" % n)
+            nc.vector.tensor_tensor(out=product[:], in0=grad[n][:], in1=step_all[:, c0:c1], op=ALU.mult)
+            scaled[n] = product
 
-        warm = psum.tile([P, CHAINS], F32, name="warm", tag="bank%d" % (BANKS - 1))
-        for rep in range(WARM_PASSES):
+        def plus_mom(n, engine):
+            j, c0, c1 = pieces[n]
+            result = keep.tile([P, c1 - c0], F32, name="result%d" % n)
+            engine.tensor_tensor(out=result[:], in0=scaled[n][:], in1=mom_sb[:, j, c0:c1], op=ALU.add)
+            nc.sync.dma_start(out=out[P * j : P * (j + 1), c0:c1], in_=result[:])
+
+        warm = psum.tile([P, K_PASS], F32, name="warm", tag="bank%d" % (BANKS - 1))
+        for i in range(WARM_PASSES):
             nc.tensor.matmul_mx(
                 out=warm[:],
-                lhsT=a_raw[0][:, 0, 0 : 2 * P].bitcast(FP4X4),
-                lhsT_scale=as_early[:, 0, 0:P],
+                lhsT=a_raw[0][:, 0, 0 : FP4_BYTES * P].bitcast(FP4X4),
+                lhsT_scale=a_direct[:, 0, 0:P],
                 rhs=a_raw[0][:, 0, :].bitcast(FP4X4),
-                rhs_scale=as_early[:, 0, 0:K_PASS],
-                start=(rep == 0),
-                stop=(rep == WARM_PASSES - 1),
+                rhs_scale=a_direct[:, 0, 0:K_PASS],
+                start=(i == 0),
+                stop=(i == WARM_PASSES - 1),
             )
-        sort_columns(0)
-        sort_columns(1)
-        nc.vector.tensor_copy(out=as_sorted[:], in_=as_spread[:].rearrange("p s (m t) -> p s t m", t=PACK))
-        w_f32 = keep.tile([P, GROUPS, PACK], F32, name="w_f32")
-        nc.vector.tensor_copy(out=w_f32[:], in_=w_bf[:])
-        sort_columns(2)
-        place_scales(0, 0, SPREAD_WIDE)
+
+        sort_group()
+        sort_group()
+        sort_spread(0)
+        weight_f32 = keep.tile([P, GROUPS, SLOTS], F32)
+        nc.vector.tensor_copy(out=weight_f32[:], in_=weight_bf[:])
+        sort_group()
+
         load_b_scales(0)
-        load_a(*A_LOADS[2])
         load_b(1)
-        place_scales(1, SPREAD_WIDE, GROUPS - EARLY_SCALE_GROUPS - SPREAD_WIDE)
+        load_spread(1)
+        load_a(5, GROUPS)
         load_b(2)
-        load_a(*A_LOADS[3])
+        load_b(3)
         load_b_scales(1)
-        for g in range(3, GROUPS):
-            load_b(g)
-        step_all = keep.tile([P, CHAINS], BF16, name="step_all")
-        nc.sync.dma_start(out=step_all[:], in_=step.partition_broadcast(P))
-        mom_sb = keep.tile([P, DIM_TILES, CHAINS], BF16, name="mom_sb")
-        nc.sync.dma_start(out=mom_sb[:], in_=mom.rearrange("(j p) c -> p j c", p=P))
+        load_b(4)
+        step_all = keep.tile([P, CHAINS], BF16)
+        mom_sb = keep.tile([P, DIM_TILES, CHAINS], BF16)
 
-        todo = [(j, g) for g in range(GROUPS) for j in range(EARLY_TILES)]
+        def load_for_the_end():
+            for g in range(len(b_words), GROUPS):
+                load_b(g)
+            nc.sync.dma_start(out=step_all[:], in_=step.partition_broadcast(P))
+            nc.sync.dma_start(out=mom_sb[:], in_=mom.rearrange("(j p) c -> p j c", p=P))
 
-        def early_pass():
-            j, g = todo[0]
-            todo.remove((j, g))
-            gradient(pieces[j], g)
+        early_passes = [(n, g) for g in range(GROUPS - 1) for n in range(EARLY_TILES)]
+
+        def next_early_pass():
+            n, g = early_passes[0]
+            early_passes.remove((n, g))
+            gradient_pass(n, g)
 
         for g in range(GROUPS):
-            for t in range(PACK):
-                margins(g, t)
-                if t == 0 and g > 0:
+            on_scalar = scalar_slots(g)
+            first_on_vector = min(t for t in range(SLOTS) if t not in on_scalar)
+            for t in range(SLOTS):
+                margin_tile(g, t)
+                if g > 0 and t == 0:
                     interleave(g - 1)
-                if t not in SCALAR_MULS[g]:
+                if t not in on_scalar:
                     weigh(g, t)
-                if t - 1 in SCALAR_MULS[g]:
+                if t - 1 in on_scalar:
                     weigh(g, t - 1)
-                if t == min(u for u in range(PACK) if u not in SCALAR_MULS[g]) and g > 0:
+                if g > 0 and t == first_on_vector:
                     quantize(g - 1)
-                if t == 1 and len(a_codes) < GROUPS and g >= SORT_FROM:
-                    sort_columns(len(a_codes))
-                if (g, t) >= (2, 2):
-                    for rep in range(WOVEN[t]):
-                        early_pass()
-            if PACK - 1 in SCALAR_MULS[g]:
-                weigh(g, PACK - 1)
+                if t == 1 and 0 < g < GROUPS - 2:
+                    sort_group()
+                if (g, t) == (2, 1):
+                    sort_spread(1)
+                    load_for_the_end()
+                if (g, t) >= (2, EXTRA_PASS_SLOT):
+                    next_early_pass()
+                    if t == EXTRA_PASS_SLOT:
+                        next_early_pass()
+            if SLOTS - 1 in on_scalar:
+                weigh(g, SLOTS - 1)
         last = GROUPS - 1
         interleave(last)
         quantize(last)
 
-        for rep in range(len(todo) - EARLY_TILES):
-            early_pass()
-        for g in range(FILL):
-            gradient(pieces[EARLY_TILES], g)
-        for j in range(EARLY_TILES):
-            gradient(pieces[j], last)
-        for g in range(FILL, GROUPS):
-            gradient(pieces[EARLY_TILES], g)
+        for i in range(len(early_passes)):
+            next_early_pass()
+        for g in range(FILL_PASSES):
+            gradient_pass(EARLY_TILES, g)
+        for n in range(EARLY_TILES):
+            gradient_pass(n, last)
+        for g in range(FILL_PASSES, GROUPS):
+            gradient_pass(EARLY_TILES, g)
 
-        scaled = {}
-
-        def scale_gradient(piece):
-            j, c0, c1 = piece
-            tmp = keep.tile([P, c1 - c0], F32, name="scaled%d_%d" % (j, c0))
-            nc.vector.tensor_tensor(out=tmp[:], in0=grad[piece][:], in1=step_all[:, c0:c1], op=ALU.mult)
-            scaled[piece] = tmp
-
-        def kick(piece, engine):
-            j, c0, c1 = piece
-            res = keep.tile([P, c1 - c0], F32, name="res%d_%d" % (j, c0))
-            engine.tensor_tensor(out=res[:], in0=scaled[piece][:], in1=mom_sb[:, j, c0:c1], op=ALU.add)
-            nc.sync.dma_start(out=out[P * j : P * (j + 1), c0:c1], in_=res[:])
-
-        for i in range(EARLY_TILES):
-            scale_gradient(pieces[i])
-            if i < GPSIMD_ADDS:
-                kick(pieces[i], nc.gpsimd)
-        for piece in pieces[EARLY_TILES + 1 :]:
+        for n in range(EARLY_TILES):
+            times_step(n)
+            if n < GPSIMD_SUMS:
+                plus_mom(n, nc.gpsimd)
+        for n in range(EARLY_TILES + 1, len(pieces)):
             for g in range(GROUPS):
-                gradient(piece, g)
-        scale_gradient(pieces[EARLY_TILES])
-        for i in range(GPSIMD_ADDS, EARLY_TILES + 1):
-            if i == M6:
-                scale_gradient(pieces[EARLY_TILES + 1])
-            kick(pieces[i], nc.vector)
-        for i in range(EARLY_TILES + 1, len(pieces) - 1):
-            scale_gradient(pieces[i + 1])
-            kick(pieces[i], nc.vector)
-        kick(pieces[-1], nc.vector)
+                gradient_pass(n, g)
+        times_step(EARLY_TILES)
+        for n in range(GPSIMD_SUMS, EARLY_TILES):
+            plus_mom(n, nc.vector)
+        for n in range(EARLY_TILES, len(pieces) - 1):
+            times_step(n + 1)
+            plus_mom(n, nc.vector)
+        plus_mom(len(pieces) - 1, nc.vector)

from contextlib import ExitStack

import concourse.mybir as mybir

OBS, DIM, CHAINS = 4096, 1024, 512
FLOPS = 2 * 2 * OBS * DIM * CHAINS

F32 = mybir.dt.float32
BF16 = mybir.dt.bfloat16
I32 = mybir.dt.int32
U32 = mybir.dt.uint32
U8 = mybir.dt.uint8
FP8X4 = mybir.dt.float8_e4m3fn_x4
FP4X4 = mybir.dt.float4_e2m1fn_x4
ACT = mybir.ActivationFunctionType
ALU = mybir.AluOpType

P = 128
QUADS = 4
SLOTS = 4
K_PASS = P * SLOTS
GROUPS = OBS // K_PASS
DIM_PASSES = DIM // K_PASS
DIM_TILES = DIM // P
BANKS = 8
FP4_BYTES = 2

EARLY_TILES = 5
EXTRA_PASS_SLOT = 2
DIRECT_GROUPS = 2
SPREAD_RUNS = [(2, 4), (6, 2)]
LAST_VECTOR_CHAINS = 320
FILL_PASSES = 4
GPSIMD_SUMS = 2
LAST_TILE_CUTS = [0, 256, 384, CHAINS]
WARM_PASSES = 3


def scalar_slots(g):
    if g == 0:
        return []
    if g + 2 < GROUPS:
        return list(range(1 + g % 2, SLOTS))
    return [0]


def tile_hmc_logistic_kick_s4_kernel(
    tc, x4_words, x4_scales, theta_words, theta_scales, x8_words, x8_scales, weight, step, mom, out
):
    nc = tc.nc
    with ExitStack() as ctx:
        keep = ctx.enter_context(tc.tile_pool(name="keep", bufs=1))
        work = ctx.enter_context(tc.tile_pool(name="work", bufs=1))
        psum = ctx.enter_context(tc.psum_pool(name="psum", bufs=1))
        ctx.enter_context(tc.manual_schedule())

        a_direct = keep.tile([P, DIM_PASSES, DIRECT_GROUPS * K_PASS], U8, align_bytes=64)
        theta_plane = keep.tile([P, DIM_PASSES, CHAINS], U8, align_bytes=64)
        spread_raw, spread_sorted, spread_plane = [], [], []
        for first, count in SPREAD_RUNS:
            raw_rows = keep.tile([P, K_PASS], U8, name="spread_raw%d" % first, align_bytes=64)
            sorted_rows = keep.tile([P, SLOTS, P], U8, name="spread_sorted%d" % first, align_bytes=64)
            run_plane = keep.tile([P, count, DIM_PASSES, SLOTS, P], U8, name="spread_plane%d" % first, align_bytes=64)
            spread_raw.append(raw_rows)
            spread_sorted.append(sorted_rows)
            spread_plane.append(run_plane)
        b_planes = []
        for half in range(GROUPS // 4):
            packed = keep.tile([P, DIM], U8, name="b_planes%d" % half, align_bytes=64)
            b_planes.append(packed)
        nc.gpsimd.memset(a_direct[:].bitcast(I32), 0)
        nc.vector.memset(theta_plane[:].bitcast(I32), 0)
        for run_plane in spread_plane:
            nc.vector.memset(run_plane[:].bitcast(I32), 0)
        nc.vector.memset(spread_raw[1][:].bitcast(I32), 0)
        for packed in b_planes:
            nc.vector.memset(packed[:].bitcast(I32), 0)

        a_raw = []
        b_words = []
        group_bytes = FP4_BYTES * K_PASS

        def load_a(first, stop):
            raw = keep.tile([P, DIM_PASSES, (stop - first) * group_bytes], U8, name="a_raw%d" % first, align_bytes=64)
            nc.sync.dma_start(
                out=raw[:].bitcast(I32),
                in_=x4_words[:, :, first * group_bytes : stop * group_bytes].rearrange("k p c -> p k c").bitcast(I32),
            )
            for i in range(stop - first):
                a_raw.append(raw[:, :, i * group_bytes : (i + 1) * group_bytes])

        def load_scale_rows(plane, rows, quads):
            for quad in quads:
                nc.sync.dma_start(
                    out=plane[32 * quad : 32 * quad + 4, :, :].bitcast(I32),
                    in_=rows[:, 4 * quad : 4 * quad + 4, :].rearrange("k r c -> r k c").bitcast(I32),
                )

        def load_spread(run):
            first, count = SPREAD_RUNS[run]
            for k in range(DIM_PASSES):
                nc.sync.dma_start(
                    out=spread_raw[run][k : 32 * count : DIM_PASSES, :].bitcast(I32),
                    in_=x4_scales[k, :, first * K_PASS : (first + count) * K_PASS]
                    .rearrange("q (h c) -> q h c", c=K_PASS)
                    .bitcast(I32),
                )

        def load_b(g):
            words = keep.tile([P, DIM], U32, name="b_words%d" % g, align_bytes=64)
            nc.sync.dma_start(out=words[:].bitcast(I32), in_=x8_words[g].rearrange("p n t -> p (n t)").bitcast(I32))
            b_words.append(words)

        def load_b_scales(half):
            for quad in range(QUADS):
                nc.sync.dma_start(
                    out=b_planes[half][32 * quad : 32 * quad + 16, :].bitcast(I32),
                    in_=x8_scales[4 * half : 4 * half + 4, 4 * quad : 4 * quad + 4, :].bitcast(I32),
                )

        load_a(0, 1)
        load_scale_rows(a_direct, x4_scales[:, :, 0 : DIRECT_GROUPS * K_PASS], range(QUADS))
        load_a(1, 3)
        load_scale_rows(theta_plane, theta_scales, range(QUADS // 2))
        theta = keep.tile([P, DIM_PASSES, FP4_BYTES * CHAINS], U8, align_bytes=64)
        nc.sync.dma_start(out=theta[:].bitcast(I32), in_=theta_words.rearrange("k p c -> p k c").bitcast(I32))
        load_scale_rows(theta_plane, theta_scales, range(QUADS // 2, QUADS))
        load_spread(0)
        weight_bf = keep.tile([P, GROUPS, SLOTS], BF16)
        nc.sync.dma_start(out=weight_bf[:], in_=weight.rearrange("(g p t) -> p g t", p=P, t=SLOTS))
        load_b(0)
        load_a(3, 5)

        a_codes = []
        a_scales = []

        def sort_group():
            g = len(a_codes)
            codes = keep.tile([P, DIM_PASSES, SLOTS, FP4_BYTES * P], U8, name="a_codes%d" % g, align_bytes=64)
            nc.vector.tensor_copy(
                out=codes[:].rearrange("p k t (m b) -> p k t m b", b=FP4_BYTES),
                in_=a_raw[g].rearrange("p k (m t b) -> p k t m b", t=SLOTS, b=FP4_BYTES),
            )
            a_codes.append(codes)
            if g < DIRECT_GROUPS:
                scales = keep.tile([P, DIM_PASSES, SLOTS, P], U8, name="a_scales%d" % g, align_bytes=64)
                rows = a_direct[:, :, g * K_PASS : (g + 1) * K_PASS]
                nc.vector.tensor_copy(out=scales[:], in_=rows.rearrange("p k (m t) -> p k t m", t=SLOTS))
                a_scales.append(scales)

        def sort_spread(run):
            count = SPREAD_RUNS[run][1]
            nc.vector.tensor_copy(
                out=spread_sorted[run][:], in_=spread_raw[run][:].rearrange("p (m t) -> p t m", t=SLOTS)
            )
            rows = 4 * count * DIM_PASSES
            for quad in range(QUADS):
                nc.sync.dma_start(
                    out=spread_plane[run][32 * quad : 32 * quad + 4].rearrange("r h k t m -> r (h k t m)").bitcast(I32),
                    in_=spread_sorted[run][rows * quad : rows * (quad + 1)].rearrange("p t m -> p (t m)").bitcast(I32),
                )
            for h in range(count):
                a_scales.append(spread_plane[run][:, h, :, :, :])

        sigmoids = {}
        r_rows = {}
        r_grouped = {}
        r_codes = []
        r_planes = []

        def margin_tile(g, t):
            i = SLOTS * g + t
            bank = i if i < BANKS else EARLY_TILES + (i - BANKS) % (BANKS - EARLY_TILES)
            z = psum.tile([P, CHAINS], F32, name="z", tag="bank%d" % bank)
            for k in range(DIM_PASSES):
                nc.tensor.matmul_mx(
                    out=z[:],
                    lhsT=a_codes[g][:, k, t, :].bitcast(FP4X4),
                    lhsT_scale=a_scales[g][:, k, t, :],
                    rhs=theta[:, k, :].bitcast(FP4X4),
                    rhs_scale=theta_plane[:, k, :],
                    start=(k == 0),
                    stop=(k == DIM_PASSES - 1),
                )
            sig = work.tile([P, CHAINS], F32, name="sig", bufs=6)
            nc.scalar.activation(out=sig[:], in_=z[:], func=ACT.Sigmoid, scale=-1.0)
            sigmoids[(g, t)] = sig

        def weigh(g, t):
            if g not in r_rows:
                rows = work.tile([P, SLOTS, CHAINS], BF16, name="r_rows", bufs=3)
                r_rows[g] = rows
            factor = weight_f32[:, g, t : t + 1]
            if t in scalar_slots(g):
                nc.scalar.activation(out=r_rows[g][:, t, :], in_=sigmoids[(g, t)][:], func=ACT.Copy, scale=factor)
            else:
                nc.vector.tensor_scalar(
                    out=r_rows[g][:, t, :], in0=sigmoids[(g, t)][:], scalar1=factor, scalar2=None, op0=ALU.mult
                )

        def interleave(g):
            grouped = work.tile([P, CHAINS, SLOTS], BF16, name="r_grouped", bufs=2, align_bytes=64)
            split = LAST_VECTOR_CHAINS if g == GROUPS - 1 else CHAINS
            nc.vector.tensor_copy(
                out=grouped[:, 0:split, :].rearrange("p (c i) t -> p c t i", i=4),
                in_=r_rows[g][:, :, 0:split].rearrange("p t (c i) -> p c t i", i=4),
            )
            if split < CHAINS:
                nc.scalar.copy(
                    out=grouped[:, split:CHAINS, :].rearrange("p (c i) t -> p c t i", i=4),
                    in_=r_rows[g][:, :, split:CHAINS].rearrange("p t (c i) -> p c t i", i=4),
                )
            r_grouped[g] = grouped

        def quantize(g):
            codes = keep.tile([P, CHAINS], U32, name="r_codes%d" % g, align_bytes=64)
            plane = keep.tile([P, CHAINS], U8, name="r_plane%d" % g, align_bytes=64)
            nc.vector.quantize_mx(
                out=codes[:].bitcast(FP8X4), scales=plane[:], in_=r_grouped[g][:].rearrange("p c t -> p (c t)")
            )
            r_codes.append(codes)
            r_planes.append(plane)

        pieces = [(j, 0, CHAINS) for j in range(DIM_TILES - 1)]
        for i in range(len(LAST_TILE_CUTS) - 1):
            pieces.append((DIM_TILES - 1, LAST_TILE_CUTS[i], LAST_TILE_CUTS[i + 1]))
        grad = {}
        scaled = {}

        def gradient_pass(n, g):
            j, c0, c1 = pieces[n]
            if g == 0:
                acc = psum.tile([P, c1 - c0], F32, name="grad", tag="bank%d" % (n % BANKS))
                grad[n] = acc
            nc.tensor.matmul_mx(
                out=grad[n][:],
                lhsT=b_words[g][:, P * j : P * (j + 1)].bitcast(FP8X4),
                lhsT_scale=b_planes[g // 4][4 * (g % 4) : P, P * j : P * (j + 1)],
                rhs=r_codes[g][:, c0:c1].bitcast(FP8X4),
                rhs_scale=r_planes[g][:, c0:c1],
                start=(g == 0),
                stop=(g == GROUPS - 1),
            )

        def times_step(n):
            j, c0, c1 = pieces[n]
            product = keep.tile([P, c1 - c0], F32, name="scaled%d" % n)
            nc.vector.tensor_tensor(out=product[:], in0=grad[n][:], in1=step_all[:, c0:c1], op=ALU.mult)
            scaled[n] = product

        def plus_mom(n, engine):
            j, c0, c1 = pieces[n]
            result = keep.tile([P, c1 - c0], F32, name="result%d" % n)
            engine.tensor_tensor(out=result[:], in0=scaled[n][:], in1=mom_sb[:, j, c0:c1], op=ALU.add)
            nc.sync.dma_start(out=out[P * j : P * (j + 1), c0:c1], in_=result[:])

        warm = psum.tile([P, K_PASS], F32, name="warm", tag="bank%d" % (BANKS - 1))
        for i in range(WARM_PASSES):
            nc.tensor.matmul_mx(
                out=warm[:],
                lhsT=a_raw[0][:, 0, 0 : FP4_BYTES * P].bitcast(FP4X4),
                lhsT_scale=a_direct[:, 0, 0:P],
                rhs=a_raw[0][:, 0, :].bitcast(FP4X4),
                rhs_scale=a_direct[:, 0, 0:K_PASS],
                start=(i == 0),
                stop=(i == WARM_PASSES - 1),
            )

        sort_group()
        sort_group()
        sort_spread(0)
        weight_f32 = keep.tile([P, GROUPS, SLOTS], F32)
        nc.vector.tensor_copy(out=weight_f32[:], in_=weight_bf[:])
        sort_group()

        load_b_scales(0)
        load_b(1)
        load_spread(1)
        load_a(5, GROUPS)
        load_b(2)
        load_b(3)
        load_b_scales(1)
        load_b(4)
        step_all = keep.tile([P, CHAINS], BF16)
        mom_sb = keep.tile([P, DIM_TILES, CHAINS], BF16)

        def load_for_the_end():
            for g in range(len(b_words), GROUPS):
                load_b(g)
            nc.sync.dma_start(out=step_all[:], in_=step.partition_broadcast(P))
            nc.sync.dma_start(out=mom_sb[:], in_=mom.rearrange("(j p) c -> p j c", p=P))

        early_passes = [(n, g) for g in range(GROUPS - 1) for n in range(EARLY_TILES)]

        def next_early_pass():
            n, g = early_passes[0]
            early_passes.remove((n, g))
            gradient_pass(n, g)

        for g in range(GROUPS):
            on_scalar = scalar_slots(g)
            first_on_vector = min(t for t in range(SLOTS) if t not in on_scalar)
            for t in range(SLOTS):
                margin_tile(g, t)
                if g > 0 and t == 0:
                    interleave(g - 1)
                if t not in on_scalar:
                    weigh(g, t)
                if t - 1 in on_scalar:
                    weigh(g, t - 1)
                if g > 0 and t == first_on_vector:
                    quantize(g - 1)
                if t == 1 and 0 < g < GROUPS - 2:
                    sort_group()
                if (g, t) == (2, 1):
                    sort_spread(1)
                    load_for_the_end()
                if (g, t) >= (2, EXTRA_PASS_SLOT):
                    next_early_pass()
                    if t == EXTRA_PASS_SLOT:
                        next_early_pass()
            if SLOTS - 1 in on_scalar:
                weigh(g, SLOTS - 1)
        last = GROUPS - 1
        interleave(last)
        quantize(last)

        for i in range(len(early_passes)):
            next_early_pass()
        for g in range(FILL_PASSES):
            gradient_pass(EARLY_TILES, g)
        for n in range(EARLY_TILES):
            gradient_pass(n, last)
        for g in range(FILL_PASSES, GROUPS):
            gradient_pass(EARLY_TILES, g)

        for n in range(EARLY_TILES):
            times_step(n)
            if n < GPSIMD_SUMS:
                plus_mom(n, nc.gpsimd)
        for n in range(EARLY_TILES + 1, len(pieces)):
            for g in range(GROUPS):
                gradient_pass(n, g)
        times_step(EARLY_TILES)
        for n in range(GPSIMD_SUMS, EARLY_TILES):
            plus_mom(n, nc.vector)
        for n in range(EARLY_TILES, len(pieces) - 1):
            times_step(n + 1)
            plus_mom(n, nc.vector)
        plus_mom(len(pieces) - 1, nc.vector)
